import numpy as np
import ml_dtypes


def mxq(x, axis, fmt="e4m3"):
    dtype, down = {"e4m3": (ml_dtypes.float8_e4m3fn, 7), "e5m2": (ml_dtypes.float8_e5m2, 14)}[fmt]
    v = np.moveaxis(np.asarray(x, np.float32).astype(ml_dtypes.bfloat16).astype(np.float64), axis, -1)
    blocks = v.reshape(v.shape[:-1] + (-1, 32))
    amax = np.abs(blocks).max(-1, keepdims=True)
    byte = np.maximum(np.where(amax > 0, np.frexp(amax)[1] - 1 + 127, 0) - down, 1)
    scale = np.exp2(byte - 127.0)
    codes = (blocks / scale).astype(np.float32).astype(dtype).astype(np.float64)
    return np.moveaxis((codes * scale).reshape(v.shape), -1, axis)


WIDE = False


def mx_kscale(k):
    if not WIDE:
        return np.ones(k)
    levels = np.array([10, -10, 5, -5, 0])
    if k % 512:
        return np.exp2(np.random.permutation(np.resize(levels, k // 32))).repeat(32)
    a = np.empty((k // 512, 16))
    for p in range(k // 512):
        a[p, :8] = np.random.permutation(np.resize(levels, 8))
        for g in range(8):
            far = levels[np.abs(levels - a[p, g]) >= 10]
            a[p, g + 8] = far[np.random.randint(len(far))]
    return np.exp2(a.ravel()).repeat(32)


def f64(x):
    return np.asarray(x).astype(np.float64)


E2M1 = np.array([0.0, 0.5, 1.0, 1.5, 2.0, 3.0, 4.0, 6.0, -0.0, -0.5, -1.0, -1.5, -2.0, -3.0, -4.0, -6.0])


def pack_weight(w, fmt):
    k, n = w.shape
    w = f64(np.asarray(w, np.float32).astype(ml_dtypes.bfloat16)).reshape(k // 32, 32, n)
    amax = np.abs(w).max(1)
    if fmt == "e4m3":
        byte = np.frexp(amax)[1] - 1 + 127 - 7
    else:
        mant, ex = np.frexp(amax / 6.0)
        byte = np.where(mant > 0.5, ex, ex - 1) + 127
    byte = np.clip(np.where(amax > 0, byte, 1), 1, 254)
    scaled = (w * np.exp2(127.0 - byte)[:, None, :]).reshape(k, n).astype(np.float32)
    by_word = np.ascontiguousarray(scaled.reshape(k // 512, 128, 4, n).transpose(0, 1, 3, 2))
    if fmt == "e4m3":
        words = by_word.astype(ml_dtypes.float8_e4m3fn).view(np.uint8)
    else:
        c = by_word.astype(ml_dtypes.float4_e2m1fn).view(np.uint8) & 0xF
        words = (c[..., 0::2] | (c[..., 1::2] << 4)).reshape(k // 512, 128, 2 * n)
    return np.ascontiguousarray(words), np.ascontiguousarray(byte.astype(np.uint8).reshape(k // 512, 16, n))


def unpack_weight(words, scales, fmt):
    g, _, n = scales.shape
    words = np.ascontiguousarray(words).reshape(g, 128, n, -1)
    if fmt == "e4m3":
        vals = words.view(ml_dtypes.float8_e4m3fn).astype(np.float64)
    else:
        nib = np.empty((g, 128, n, 4), np.uint8)
        nib[..., 0::2] = words & 0xF
        nib[..., 1::2] = words >> 4
        vals = E2M1[nib]
    vals = vals * np.repeat(np.exp2(scales.astype(np.float64) - 127.0), 8, axis=1)[..., None]
    return vals.transpose(0, 1, 3, 2).reshape(g * 512, n)


def bf(x):
    return np.asarray(x, np.float32).astype(ml_dtypes.bfloat16)


def planes(Y):
    r, m = Y.shape
    b = f64(bf(Y)).reshape(r // 32, 32, m)
    amax = np.abs(b).max(1)
    byte = np.clip(np.where(amax > 0, np.frexp(amax)[1] - 1 + 127 - 7, 1), 1, 254)
    codes = (b * np.exp2(127.0 - byte)[:, None, :]).reshape(r, m).astype(np.float32).astype(ml_dtypes.float8_e4m3fn).view(np.uint8)
    words = codes.reshape(r // 512, 128, 4, m).transpose(0, 1, 3, 2)
    return np.ascontiguousarray(words), np.ascontiguousarray(byte.astype(np.uint8).reshape(r // 512, 16, m))


K, L, T, N = 1024, 1024, 512, 512


def setup_inputs():
    n = np.random.standard_normal
    fk = mx_kscale(K)
    fl = mx_kscale(L)
    xap = pack_weight(n((K, T)) / fk[:, None], "e2m1")
    wap = pack_weight(n((K, N)) * 1 / np.sqrt(K) * fk[:, None], "e4m3")
    wqp = pack_weight(n((L, N)) * 1 / np.sqrt(L) * fl[:, None], "e2m1")
    return {
        "xa_words": xap[0],
        "xa_scales": xap[1],
        "wa_words": wap[0],
        "wa_scales": wap[1],
        "xq": (n((L, T)) / fl[:, None]).astype(np.float32),
        "wq_words": wqp[0],
        "wq_scales": wqp[1],
        "wc": (n((K, N)) * 1 / np.sqrt(K) * fk[:, None]).astype(np.float32),
    }


def reference(xa_words, xa_scales, wa_words, wa_scales, xq, wq_words, wq_scales, wc):
    xau = unpack_weight(xa_words, xa_scales, "e2m1")
    wau = unpack_weight(wa_words, wa_scales, "e4m3")
    wqu = unpack_weight(wq_words, wq_scales, "e2m1")
    xqq = mxq(f64(xq), 0, "e4m3")
    p = wau.T @ xau + wqu.T @ xqq
    wcq = mxq(f64(wc), 0, "e4m3")
    r = wcq.T @ xau
    y = np.maximum(p, 1.4 * r) - 0.25 * (p + r)
    words, scales = planes(y)
    return y, words, scales

@@ -1,0 +1,302 @@
+from contextlib import ExitStack
+
+import concourse.mybir as mybir
+from concourse.masks import make_identity
+
+K, L, T, N = 1024, 1024, 512, 512
+FLOPS = 2 * N * T * (2 * K + L)
+
+F32 = mybir.dt.float32
+BF16 = mybir.dt.bfloat16
+I32 = mybir.dt.int32
+U32 = mybir.dt.uint32
+U8 = mybir.dt.uint8
+FP8X4 = mybir.dt.float8_e4m3fn_x4
+FP4X4 = mybir.dt.float4_e2m1fn_x4
+ALU = mybir.AluOpType
+COPY = mybir.ActivationFunctionType.Copy
+
+P = 128
+PACK = 4
+K_PASS = P * PACK
+PASSES = K // K_PASS
+CHUNK = 128
+CHUNKS = T // CHUNK
+HALF = N // 2
+
+
+def interleave_views(grouped, raw, lo, hi):
+    dst = grouped[:, lo:hi, :].rearrange("p (c i) j -> p c j i", i=4)
+    src = raw[:, :, lo:hi].rearrange("p j (c i) -> p c j i", i=4)
+    return dst, src
+
+
+def tile_mix_larger_of_two_sums_pl_kernel(
+    tc, xa_words, xa_scales, wa_words, wa_scales, xq, wq_words, wq_scales, wc, out_0, out_1, out_2
+):
+    nc = tc.nc
+    with ExitStack() as ctx:
+        sb = ctx.enter_context(tc.tile_pool(name="sb", bufs=1))
+        ps = ctx.enter_context(tc.psum_pool(name="ps", bufs=1))
+        ctx.enter_context(tc.manual_schedule())
+
+        def tile(name, shape, dtype):
+            return sb.tile(shape, dtype, name=name, align_bytes=64)
+
+        xa_w = tile("xa_w", [P, PASSES, 2 * T], U8)
+        wq_w = tile("wq_w", [P, PASSES, 2 * N], U8)
+        wa_w = [tile("wa_w%d" % z, [P, N], U32) for z in range(PASSES)]
+        xa_s = tile("xa_s", [P, PASSES, T], U8)
+        wa_s = tile("wa_s", [P, PASSES, N], U8)
+        wq_s = tile("wq_s", [P, PASSES, N], U8)
+        ident = tile("ident", [P, P], F32)
+
+        wc_cols = [(0, 0, N), (1, 0, HALF), (1, HALF, N)]
+        wc_raw = [tile("wc_raw%d" % i, [P, PACK, hi - lo], F32) for i, (z, lo, hi) in enumerate(wc_cols)]
+        wc_bf = [tile("wc_bf%d" % i, [P, hi - lo, PACK], BF16) for i, (z, lo, hi) in enumerate(wc_cols)]
+        wc_w = [tile("wc_w%d" % z, [P, N], U32) for z in range(PASSES)]
+        wc_s = [tile("wc_s%d" % z, [P, N], U8) for z in range(PASSES)]
+        pieces = [(c, z) for c in range(CHUNKS) for z in range(PASSES)]
+        xq_raw = {k: tile("xq_raw%d%d" % k, [P, PACK, CHUNK], F32) for k in pieces}
+        xq_bf = {k: tile("xq_bf%d%d" % k, [P, CHUNK, PACK], BF16) for k in pieces}
+        xq_w = {k: tile("xq_w%d%d" % k, [P, CHUNK], U32) for k in pieces}
+        xq_s = {k: tile("xq_s%d%d" % k, [P, CHUNK], U8) for k in pieces}
+        rn = [tile("rn%d" % c, [P, PACK, P], F32) for c in range(CHUNKS)]
+        larger = [tile("larger%d" % c, [P, PACK, P], F32) for c in range(CHUNKS)]
+        both = [tile("both%d" % c, [P, PACK, P], F32) for c in range(CHUNKS)]
+        y = [tile("y%d" % c, [P, PACK, CHUNK], F32) for c in range(CHUNKS)]
+        y_bf = [tile("y_bf%d" % c, [P, CHUNK, PACK], BF16) for c in range(CHUNKS)]
+        y_w = tile("y_w", [P, T], U32)
+        y_s = tile("y_s", [P, T], U8)
+
+        p_acc = [ps.tile([P, N], F32, name="p_acc%d" % c, tag="p%d" % c) for c in range(CHUNKS)]
+        r_acc = [ps.tile([P, N], F32, name="r_acc%d" % c, tag="r%d" % c) for c in range(CHUNKS)]
+        y_acc = {}
+
+        for plane in (xa_s, wa_s, wq_s):
+            nc.vector.memset(plane[:].bitcast(I32), 0)
+        make_identity(nc, ident[:])
+
+        def load_scales(queue, plane, scales, r):
+            queue.dma_start(
+                out=plane[r:P:32, :, :].bitcast(I32),
+                in_=scales[:, r:16:4, :].rearrange("z q n -> q z n").bitcast(I32),
+            )
+
+        def load_fp4(dst, words):
+            nc.sync.dma_start(out=dst[:].bitcast(I32), in_=words.rearrange("z p b -> p z b").bitcast(I32))
+
+        def load_wa(z):
+            nc.sync.dma_start(
+                out=wa_w[z][:].bitcast(I32), in_=wa_words[z].rearrange("p n t -> p (n t)").bitcast(I32)
+            )
+
+        def load_rows(dst, src, z, lo, hi):
+            rows = src[z * K_PASS : (z + 1) * K_PASS, lo:hi]
+            nc.sync.dma_start(out=dst[:], in_=rows.rearrange("(p j) w -> p j w", j=PACK))
+
+        def load_xq(c, z):
+            load_rows(xq_raw[c, z], xq, z, c * CHUNK, (c + 1) * CHUNK)
+
+        load_fp4(xa_w, xa_words)
+        for r in range(4):
+            load_scales(nc.scalar, xa_s, xa_scales, r)
+        load_wa(0)
+        load_rows(wc_raw[0], wc, *wc_cols[0])
+        for r in range(4):
+            load_scales(nc.scalar, wa_s, wa_scales, r)
+        load_wa(1)
+        load_rows(wc_raw[1], wc, *wc_cols[1])
+        load_rows(wc_raw[2], wc, *wc_cols[2])
+        load_xq(0, 0)
+        load_xq(0, 1)
+        load_fp4(wq_w, wq_words)
+        for r in range(4):
+            load_scales(nc.sync, wq_s, wq_scales, r)
+        for c in range(1, CHUNKS):
+            for z in range(PASSES):
+                load_xq(c, z)
+
+        def round_on_vector(grouped, raw, lo, hi):
+            dst, src = interleave_views(grouped, raw, lo, hi)
+            nc.vector.tensor_copy(out=dst, in_=src)
+
+        def round_on_scalar(grouped, raw, lo, hi):
+            dst, src = interleave_views(grouped, raw, lo, hi)
+            nc.scalar.activation(out=dst, in_=src, func=COPY)
+
+        def quantise(words, scales, grouped):
+            nc.vector.quantize_mx(
+                out=words.bitcast(FP8X4), scales=scales, in_=grouped[:].rearrange("p w j -> p (w j)")
+            )
+
+        def round_wc(i):
+            z, lo, hi = wc_cols[i]
+            width = hi - lo
+            split = width * 11 // 16
+            round_on_scalar(wc_bf[i], wc_raw[i], split, width)
+            round_on_vector(wc_bf[i], wc_raw[i], 0, split)
+
+        def quantise_wc(i):
+            z, lo, hi = wc_cols[i]
+            quantise(wc_w[z][:, lo:hi], wc_s[z][:, lo:hi], wc_bf[i])
+
+        def quantise_xq(c, z):
+            quantise(xq_w[c, z][:], xq_s[c, z][:], xq_bf[c, z])
+
+        def xa_pass(acc, c, z, words, scales, start, stop):
+            nc.tensor.matmul_mx(
+                out=acc[:],
+                lhsT=xa_w[:, z, 2 * c * CHUNK : 2 * (c + 1) * CHUNK].bitcast(FP4X4),
+                lhsT_scale=xa_s[:, z, c * CHUNK : (c + 1) * CHUNK],
+                rhs=words.bitcast(FP8X4),
+                rhs_scale=scales,
+                start=start,
+                stop=stop,
+            )
+
+        def xq_pass(c, z):
+            nc.tensor.matmul_mx(
+                out=p_acc[c][:],
+                lhsT=xq_w[c, z][:].bitcast(FP8X4),
+                lhsT_scale=xq_s[c, z][:],
+                rhs=wq_w[:, z, :].bitcast(FP4X4),
+                rhs_scale=wq_s[:, z, :],
+                start=False,
+                stop=(z == PASSES - 1),
+            )
+
+        def dealt(acc):
+            return acc[:].rearrange("t (m r) -> t r m", r=PACK)
+
+        def copy_r(c):
+            nc.scalar.activation(out=rn[c][:], in_=dealt(r_acc[c]), func=COPY, scale=-0.25)
+
+        def take_larger(c):
+            nc.vector.scalar_tensor_tensor(
+                out=larger[c][:], in0=rn[c][:], scalar=-5.6, in1=dealt(p_acc[c]), op0=ALU.mult, op1=ALU.max
+            )
+
+        def take_both(c):
+            nc.vector.scalar_tensor_tensor(
+                out=both[c][:], in0=dealt(p_acc[c]), scalar=-0.25, in1=rn[c][:], op0=ALU.mult, op1=ALU.add
+            )
+
+        def turn(c, i):
+            if i == 0:
+                y_acc[c] = ps.tile([P, PACK, CHUNK], F32, name="y_acc%d" % c, tag="r%d" % c)
+            term = (larger, both)[i][c]
+            for r in range(PACK):
+                nc.tensor.matmul(
+                    out=y_acc[c][:, r, :],
+                    lhsT=term[:, r, :],
+                    rhs=ident[:],
+                    is_transpose=True,
+                    start=(i == 0 and r == 0),
+                    stop=(i == 1 and r == PACK - 1),
+                )
+
+        out_rows = out_0.rearrange("(p r) t -> p r t", r=PACK)
+        out_words = out_1[0].rearrange("p c r -> p (c r)").bitcast(I32)
+
+        def copy_y(c):
+            nc.scalar.copy(out=y[c][:], in_=y_acc[c][:])
+            nc.sync.dma_start(out=out_rows[:, :, c * CHUNK : (c + 1) * CHUNK], in_=y[c][:])
+
+        def round_y(c):
+            round_on_vector(y_bf[c], y[c], 0, CHUNK)
+
+        def quantise_y(c):
+            cols = slice(c * CHUNK, (c + 1) * CHUNK)
+            quantise(y_w[:, cols], y_s[:, cols], y_bf[c])
+
+        def round_xq(c, z):
+            round_on_scalar(xq_bf[c, z], xq_raw[c, z], 0, CHUNK)
+
+        def a_pass(c, z):
+            xa_pass(p_acc[c], c, z, wa_w[z][:], wa_s[:, z, :], z == 0, False)
+
+        def r_pass(c, z):
+            xa_pass(r_acc[c], c, z, wc_w[z][:], wc_s[z][:], z == 0, z == 1)
+
+        def round_xq_v(c, z):
+            round_on_vector(xq_bf[c, z], xq_raw[c, z], 0, CHUNK)
+
+        for c in range(CHUNKS):
+            a_pass(c, 0)
+        round_wc(0)
+        quantise_wc(0)
+        for c in range(CHUNKS):
+            r_pass(c, 0)
+        round_wc(1)
+        quantise_wc(1)
+        for c in range(CHUNKS):
+            a_pass(c, 1)
+        round_wc(2)
+        quantise_wc(2)
+        r_pass(0, 1)
+        r_pass(1, 1)
+        copy_r(0)
+        copy_r(1)
+        round_xq_v(0, 0)
+        round_xq_v(0, 1)
+        for z in range(PASSES):
+            quantise_xq(0, z)
+            xq_pass(0, z)
+        r_pass(2, 1)
+        r_pass(3, 1)
+        round_xq(1, 0)
+        round_xq(1, 1)
+        take_larger(0)
+        take_both(0)
+        quantise_xq(1, 0)
+        quantise_xq(1, 1)
+        turn(0, 0)
+        xq_pass(1, 0)
+        xq_pass(1, 1)
+        turn(0, 1)
+        copy_r(2)
+        round_xq(2, 0)
+        round_xq_v(2, 1)
+        copy_r(3)
+        quantise_xq(2, 0)
+        take_larger(1)
+        quantise_xq(2, 1)
+        take_both(1)
+        xq_pass(2, 0)
+        xq_pass(2, 1)
+        turn(1, 0)
+        turn(1, 1)
+        round_xq(3, 0)
+        round_xq(3, 1)
+        copy_y(0)
+        take_larger(2)
+        quantise_xq(3, 0)
+        quantise_xq(3, 1)
+        take_both(2)
+        xq_pass(3, 0)
+        xq_pass(3, 1)
+        turn(2, 0)
+        turn(2, 1)
+        copy_y(1)
+        round_y(0)
+        take_larger(3)
+        take_both(3)
+        turn(3, 0)
+        turn(3, 1)
+        copy_y(2)
+        copy_y(3)
+        round_y(1)
+        quantise_y(0)
+        round_y(2)
+        quantise_y(1)
+        quantise_y(2)
+        nc.sync.dma_start(out=out_words[:, : 3 * CHUNK], in_=y_w[:, : 3 * CHUNK].bitcast(I32))
+        round_y(3)
+        quantise_y(3)
+        nc.sync.dma_start(out=out_words[:, 3 * CHUNK :], in_=y_w[:, 3 * CHUNK :].bitcast(I32))
+        for q in range(4):
+            queue = nc.scalar if q % 2 == 0 else nc.sync
+            queue.dma_start(
+                out=out_2[0, 4 * q : 4 * q + 4, :].bitcast(I32), in_=y_s[32 * q : 32 * q + 4, :].bitcast(I32)
+            )

@@ -98,24 +98,19 @@ def tile_mix_larger_of_two_sums_pl_kernel(
         def load_xq(c, z):
             load_rows(xq_raw[c, z], xq, z, c * CHUNK, (c + 1) * CHUNK)
 
-        load_fp4(xa_w, xa_words)
-        for r in range(4):
-            load_scales(nc.scalar, xa_s, xa_scales, r)
-        load_wa(0)
         load_rows(wc_raw[0], wc, *wc_cols[0])
-        for r in range(4):
-            load_scales(nc.scalar, wa_s, wa_scales, r)
-        load_wa(1)
+        load_fp4(xa_w, xa_words)
+        [load_scales(nc.sync, xa_s, xa_scales, r) for r in range(4)]
         load_rows(wc_raw[1], wc, *wc_cols[1])
         load_rows(wc_raw[2], wc, *wc_cols[2])
+        load_wa(0)
+        [load_scales(nc.sync, wa_s, wa_scales, r) for r in range(4)]
+        load_wa(1)
         load_xq(0, 0)
         load_xq(0, 1)
         load_fp4(wq_w, wq_words)
-        for r in range(4):
-            load_scales(nc.sync, wq_s, wq_scales, r)
-        for c in range(1, CHUNKS):
-            for z in range(PASSES):
-                load_xq(c, z)
+        [load_scales(nc.sync, wq_s, wq_scales, r) for r in range(4)]
+        [load_xq(c, z) for c in range(1, CHUNKS) for z in range(PASSES)]
 
         def round_on_vector(grouped, raw, lo, hi):
             dst, src = interleave_views(grouped, raw, lo, hi)
@@ -219,75 +214,76 @@ def tile_mix_larger_of_two_sums_pl_kernel(
         def r_pass(c, z):
             xa_pass(r_acc[c], c, z, wc_w[z][:], wc_s[z][:], z == 0, z == 1)
 
+        def round_y_s(c):
+            round_on_scalar(y_bf[c], y[c], 0, CHUNK)
+
         def round_xq_v(c, z):
             round_on_vector(xq_bf[c, z], xq_raw[c, z], 0, CHUNK)
 
-        for c in range(CHUNKS):
-            a_pass(c, 0)
         round_wc(0)
         quantise_wc(0)
-        for c in range(CHUNKS):
-            r_pass(c, 0)
+        [r_pass(c, 0) for c in range(CHUNKS)]
         round_wc(1)
         quantise_wc(1)
-        for c in range(CHUNKS):
-            a_pass(c, 1)
         round_wc(2)
         quantise_wc(2)
-        r_pass(0, 1)
-        r_pass(1, 1)
-        copy_r(0)
-        copy_r(1)
+        a_pass(0, 0)
+        [r_pass(c, 1) for c in range(CHUNKS)]
+        [copy_r(c) for c in range(CHUNKS)]
+        a_pass(0, 1)
+        a_pass(1, 0)
+        a_pass(1, 1)
         round_xq_v(0, 0)
         round_xq_v(0, 1)
-        for z in range(PASSES):
-            quantise_xq(0, z)
-            xq_pass(0, z)
-        r_pass(2, 1)
-        r_pass(3, 1)
+        quantise_xq(0, 0)
+        quantise_xq(0, 1)
+        xq_pass(0, 0)
+        xq_pass(0, 1)
+        a_pass(2, 0)
+        a_pass(2, 1)
+        a_pass(3, 0)
+        a_pass(3, 1)
         round_xq(1, 0)
         round_xq(1, 1)
         take_larger(0)
-        take_both(0)
         quantise_xq(1, 0)
-        quantise_xq(1, 1)
-        turn(0, 0)
         xq_pass(1, 0)
+        take_both(0)
+        quantise_xq(1, 1)
         xq_pass(1, 1)
+        turn(0, 0)
         turn(0, 1)
-        copy_r(2)
         round_xq(2, 0)
-        round_xq_v(2, 1)
-        copy_r(3)
+        round_xq(2, 1)
         quantise_xq(2, 0)
+        xq_pass(2, 0)
         take_larger(1)
         quantise_xq(2, 1)
-        take_both(1)
-        xq_pass(2, 0)
         xq_pass(2, 1)
+        take_both(1)
         turn(1, 0)
         turn(1, 1)
         round_xq(3, 0)
         round_xq(3, 1)
         copy_y(0)
-        take_larger(2)
         quantise_xq(3, 0)
-        quantise_xq(3, 1)
-        take_both(2)
         xq_pass(3, 0)
+        take_larger(2)
+        quantise_xq(3, 1)
         xq_pass(3, 1)
+        take_both(2)
         turn(2, 0)
         turn(2, 1)
         copy_y(1)
-        round_y(0)
+        round_y_s(0)
         take_larger(3)
-        take_both(3)
         turn(3, 0)
+        take_both(3)
         turn(3, 1)
         copy_y(2)
-        copy_y(3)
         round_y(1)
         quantise_y(0)
+        copy_y(3)
         round_y(2)
         quantise_y(1)
         quantise_y(2)

@@ -45,7 +45,7 @@ def tile_mix_larger_of_two_sums_pl_kernel(
 
         xa_w = tile("xa_w", [P, PASSES, 2 * T], U8)
         wq_w = tile("wq_w", [P, PASSES, 2 * N], U8)
-        wa_w = [tile("wa_w%d" % z, [P, N], U32) for z in range(PASSES)]
+        wa_w = tile("wa_w", [P, PASSES, N], U32)
         xa_s = tile("xa_s", [P, PASSES, T], U8)
         wa_s = tile("wa_s", [P, PASSES, N], U8)
         wq_s = tile("wq_s", [P, PASSES, N], U8)
@@ -73,9 +73,8 @@ def tile_mix_larger_of_two_sums_pl_kernel(
         r_acc = [ps.tile([P, N], F32, name="r_acc%d" % c, tag="r%d" % c) for c in range(CHUNKS)]
         y_acc = {}
 
-        for plane in (xa_s, wa_s, wq_s):
+        for plane in (wq_s, xa_s, wa_s):
             nc.vector.memset(plane[:].bitcast(I32), 0)
-        make_identity(nc, ident[:])
 
         def load_scales(queue, plane, scales, r):
             queue.dma_start(
@@ -86,11 +85,6 @@ def tile_mix_larger_of_two_sums_pl_kernel(
         def load_fp4(dst, words):
             nc.sync.dma_start(out=dst[:].bitcast(I32), in_=words.rearrange("z p b -> p z b").bitcast(I32))
 
-        def load_wa(z):
-            nc.sync.dma_start(
-                out=wa_w[z][:].bitcast(I32), in_=wa_words[z].rearrange("p n t -> p (n t)").bitcast(I32)
-            )
-
         def load_rows(dst, src, z, lo, hi):
             rows = src[z * K_PASS : (z + 1) * K_PASS, lo:hi]
             nc.sync.dma_start(out=dst[:], in_=rows.rearrange("(p j) w -> p j w", j=PACK))
@@ -98,18 +92,19 @@ def tile_mix_larger_of_two_sums_pl_kernel(
         def load_xq(c, z):
             load_rows(xq_raw[c, z], xq, z, c * CHUNK, (c + 1) * CHUNK)
 
+        [load_scales(nc.gpsimd, wq_s, wq_scales, r) for r in range(4)]
+        make_identity(nc, ident[:])
         load_rows(wc_raw[0], wc, *wc_cols[0])
         load_fp4(xa_w, xa_words)
         [load_scales(nc.sync, xa_s, xa_scales, r) for r in range(4)]
         load_rows(wc_raw[1], wc, *wc_cols[1])
         load_rows(wc_raw[2], wc, *wc_cols[2])
-        load_wa(0)
-        [load_scales(nc.sync, wa_s, wa_scales, r) for r in range(4)]
-        load_wa(1)
+        load_scales(nc.sync, wa_s, wa_scales, 0)
+        nc.sync.dma_start(out=wa_w[:].bitcast(I32), in_=wa_words.rearrange("z p n t -> p z (n t)").bitcast(I32))
+        [load_scales(nc.sync, wa_s, wa_scales, r) for r in range(1, 4)]
         load_xq(0, 0)
         load_xq(0, 1)
         load_fp4(wq_w, wq_words)
-        [load_scales(nc.sync, wq_s, wq_scales, r) for r in range(4)]
         [load_xq(c, z) for c in range(1, CHUNKS) for z in range(PASSES)]
 
         def round_on_vector(grouped, raw, lo, hi):
@@ -198,18 +193,23 @@ def tile_mix_larger_of_two_sums_pl_kernel(
             nc.scalar.copy(out=y[c][:], in_=y_acc[c][:])
             nc.sync.dma_start(out=out_rows[:, :, c * CHUNK : (c + 1) * CHUNK], in_=y[c][:])
 
-        def round_y(c):
-            round_on_vector(y_bf[c], y[c], 0, CHUNK)
+        def round_y(c, lo=0, hi=CHUNK):
+            round_on_vector(y_bf[c], y[c], lo, hi)
 
-        def quantise_y(c):
-            cols = slice(c * CHUNK, (c + 1) * CHUNK)
-            quantise(y_w[:, cols], y_s[:, cols], y_bf[c])
+        def quantise_y(c, lo=0, hi=CHUNK):
+            cols = slice(c * CHUNK + lo, c * CHUNK + hi)
+            quantise(y_w[:, cols], y_s[:, cols], y_bf[c][:, lo:hi, :])
+
+        def copy_y_halves(c):
+            for lo in (0, CHUNK // 2):
+                cols = slice(lo, lo + CHUNK // 2)
+                nc.scalar.copy(out=y[c][:, :, cols], in_=y_acc[c][:, :, cols])
 
         def round_xq(c, z):
             round_on_scalar(xq_bf[c, z], xq_raw[c, z], 0, CHUNK)
 
         def a_pass(c, z):
-            xa_pass(p_acc[c], c, z, wa_w[z][:], wa_s[:, z, :], z == 0, False)
+            xa_pass(p_acc[c], c, z, wa_w[:, z, :], wa_s[:, z, :], z == 0, False)
 
         def r_pass(c, z):
             xa_pass(r_acc[c], c, z, wc_w[z][:], wc_s[z][:], z == 0, z == 1)
@@ -227,9 +227,9 @@ def tile_mix_larger_of_two_sums_pl_kernel(
         quantise_wc(1)
         round_wc(2)
         quantise_wc(2)
-        a_pass(0, 0)
         [r_pass(c, 1) for c in range(CHUNKS)]
         [copy_r(c) for c in range(CHUNKS)]
+        a_pass(0, 0)
         a_pass(0, 1)
         a_pass(1, 0)
         a_pass(1, 1)
@@ -242,7 +242,6 @@ def tile_mix_larger_of_two_sums_pl_kernel(
         a_pass(2, 0)
         a_pass(2, 1)
         a_pass(3, 0)
-        a_pass(3, 1)
         round_xq(1, 0)
         round_xq(1, 1)
         take_larger(0)
@@ -261,6 +260,7 @@ def tile_mix_larger_of_two_sums_pl_kernel(
         quantise_xq(2, 1)
         xq_pass(2, 1)
         take_both(1)
+        a_pass(3, 1)
         turn(1, 0)
         turn(1, 1)
         round_xq(3, 0)
@@ -283,14 +283,17 @@ def tile_mix_larger_of_two_sums_pl_kernel(
         copy_y(2)
         round_y(1)
         quantise_y(0)
-        copy_y(3)
+        copy_y_halves(3)
         round_y(2)
         quantise_y(1)
+        nc.sync.dma_start(out=out_words[:, : 2 * CHUNK], in_=y_w[:, : 2 * CHUNK].bitcast(I32))
+        nc.sync.dma_start(out=out_rows[:, :, 3 * CHUNK :], in_=y[3][:])
         quantise_y(2)
-        nc.sync.dma_start(out=out_words[:, : 3 * CHUNK], in_=y_w[:, : 3 * CHUNK].bitcast(I32))
-        round_y(3)
-        quantise_y(3)
-        nc.sync.dma_start(out=out_words[:, 3 * CHUNK :], in_=y_w[:, 3 * CHUNK :].bitcast(I32))
+        round_y(3, 0, 64)
+        round_y(3, 64, 128)
+        quantise_y(3, 0, 64)
+        quantise_y(3, 64, 128)
+        nc.sync.dma_start(out=out_words[:, 2 * CHUNK :], in_=y_w[:, 2 * CHUNK :].bitcast(I32))
         for q in range(4):
             queue = nc.scalar if q % 2 == 0 else nc.sync
             queue.dma_start(

@@ -20,15 +20,15 @@ P = 128
 PACK = 4
 K_PASS = P * PACK
 PASSES = K // K_PASS
+QUADRANT = 32
+SCALE_ROWS = 4
 CHUNK = 128
 CHUNKS = T // CHUNK
-HALF = N // 2
+LAST = CHUNKS - 1
+LINE = 4
 
-
-def interleave_views(grouped, raw, lo, hi):
-    dst = grouped[:, lo:hi, :].rearrange("p (c i) j -> p c j i", i=4)
-    src = raw[:, :, lo:hi].rearrange("p j (c i) -> p c j i", i=4)
-    return dst, src
+WC_PIECES = ((0, 0, N), (1, 0, N // 2), (1, N // 2, N))
+VECTOR_SHARE = 11 / 16
 
 
 def tile_mix_larger_of_two_sums_pl_kernel(
@@ -36,12 +36,12 @@ def tile_mix_larger_of_two_sums_pl_kernel(
 ):
     nc = tc.nc
     with ExitStack() as ctx:
-        sb = ctx.enter_context(tc.tile_pool(name="sb", bufs=1))
-        ps = ctx.enter_context(tc.psum_pool(name="ps", bufs=1))
+        sbuf = ctx.enter_context(tc.tile_pool(name="sbuf", bufs=1))
+        psum = ctx.enter_context(tc.psum_pool(name="psum", bufs=1))
         ctx.enter_context(tc.manual_schedule())
 
         def tile(name, shape, dtype):
-            return sb.tile(shape, dtype, name=name, align_bytes=64)
+            return sbuf.tile(shape, dtype, name=name, align_bytes=64)
 
         xa_w = tile("xa_w", [P, PASSES, 2 * T], U8)
         wq_w = tile("wq_w", [P, PASSES, 2 * N], U8)
@@ -49,19 +49,19 @@ def tile_mix_larger_of_two_sums_pl_kernel(
         xa_s = tile("xa_s", [P, PASSES, T], U8)
         wa_s = tile("wa_s", [P, PASSES, N], U8)
         wq_s = tile("wq_s", [P, PASSES, N], U8)
-        ident = tile("ident", [P, P], F32)
+        identity = tile("identity", [P, P], F32)
 
-        wc_cols = [(0, 0, N), (1, 0, HALF), (1, HALF, N)]
-        wc_raw = [tile("wc_raw%d" % i, [P, PACK, hi - lo], F32) for i, (z, lo, hi) in enumerate(wc_cols)]
-        wc_bf = [tile("wc_bf%d" % i, [P, hi - lo, PACK], BF16) for i, (z, lo, hi) in enumerate(wc_cols)]
+        wc_raw = [tile("wc_raw%d" % i, [P, PACK, hi - lo], F32) for i, (z, lo, hi) in enumerate(WC_PIECES)]
+        wc_bf = [tile("wc_bf%d" % i, [P, hi - lo, PACK], BF16) for i, (z, lo, hi) in enumerate(WC_PIECES)]
         wc_w = [tile("wc_w%d" % z, [P, N], U32) for z in range(PASSES)]
         wc_s = [tile("wc_s%d" % z, [P, N], U8) for z in range(PASSES)]
-        pieces = [(c, z) for c in range(CHUNKS) for z in range(PASSES)]
-        xq_raw = {k: tile("xq_raw%d%d" % k, [P, PACK, CHUNK], F32) for k in pieces}
-        xq_bf = {k: tile("xq_bf%d%d" % k, [P, CHUNK, PACK], BF16) for k in pieces}
-        xq_w = {k: tile("xq_w%d%d" % k, [P, CHUNK], U32) for k in pieces}
-        xq_s = {k: tile("xq_s%d%d" % k, [P, CHUNK], U8) for k in pieces}
-        rn = [tile("rn%d" % c, [P, PACK, P], F32) for c in range(CHUNKS)]
+        xq_pieces = [(c, z) for c in range(CHUNKS) for z in range(PASSES)]
+        xq_raw = {cz: tile("xq_raw%d%d" % cz, [P, PACK, CHUNK], F32) for cz in xq_pieces}
+        xq_bf = {cz: tile("xq_bf%d%d" % cz, [P, CHUNK, PACK], BF16) for cz in xq_pieces}
+        xq_w = {cz: tile("xq_w%d%d" % cz, [P, CHUNK], U32) for cz in xq_pieces}
+        xq_s = {cz: tile("xq_s%d%d" % cz, [P, CHUNK], U8) for cz in xq_pieces}
+
+        r_quarter = [tile("r_quarter%d" % c, [P, PACK, P], F32) for c in range(CHUNKS)]
         larger = [tile("larger%d" % c, [P, PACK, P], F32) for c in range(CHUNKS)]
         both = [tile("both%d" % c, [P, PACK, P], F32) for c in range(CHUNKS)]
         y = [tile("y%d" % c, [P, PACK, CHUNK], F32) for c in range(CHUNKS)]
@@ -69,83 +69,68 @@ def tile_mix_larger_of_two_sums_pl_kernel(
         y_w = tile("y_w", [P, T], U32)
         y_s = tile("y_s", [P, T], U8)
 
-        p_acc = [ps.tile([P, N], F32, name="p_acc%d" % c, tag="p%d" % c) for c in range(CHUNKS)]
-        r_acc = [ps.tile([P, N], F32, name="r_acc%d" % c, tag="r%d" % c) for c in range(CHUNKS)]
+        p_acc = [psum.tile([P, N], F32, name="p_acc%d" % c, tag="p%d" % c) for c in range(CHUNKS)]
+        r_acc = [psum.tile([P, N], F32, name="r_acc%d" % c, tag="r%d" % c) for c in range(CHUNKS)]
         y_acc = {}
 
-        for plane in (wq_s, xa_s, wa_s):
-            nc.vector.memset(plane[:].bitcast(I32), 0)
-
-        def load_scales(queue, plane, scales, r):
+        def load_scales(queue, dst, scales, s):
             queue.dma_start(
-                out=plane[r:P:32, :, :].bitcast(I32),
-                in_=scales[:, r:16:4, :].rearrange("z q n -> q z n").bitcast(I32),
+                out=dst[s:P:QUADRANT, :, :].bitcast(I32),
+                in_=scales[:, s::SCALE_ROWS, :].rearrange("z q n -> q z n").bitcast(I32),
             )
 
-        def load_fp4(dst, words):
-            nc.sync.dma_start(out=dst[:].bitcast(I32), in_=words.rearrange("z p b -> p z b").bitcast(I32))
+        def load_words(dst, words):
+            nc.sync.dma_start(out=dst[:].bitcast(I32), in_=words.bitcast(I32))
 
         def load_rows(dst, src, z, lo, hi):
             rows = src[z * K_PASS : (z + 1) * K_PASS, lo:hi]
-            nc.sync.dma_start(out=dst[:], in_=rows.rearrange("(p j) w -> p j w", j=PACK))
+            nc.sync.dma_start(out=dst[:], in_=rows.rearrange("(i j) w -> i j w", j=PACK))
 
         def load_xq(c, z):
             load_rows(xq_raw[c, z], xq, z, c * CHUNK, (c + 1) * CHUNK)
 
-        [load_scales(nc.gpsimd, wq_s, wq_scales, r) for r in range(4)]
-        make_identity(nc, ident[:])
-        load_rows(wc_raw[0], wc, *wc_cols[0])
-        load_fp4(xa_w, xa_words)
-        [load_scales(nc.sync, xa_s, xa_scales, r) for r in range(4)]
-        load_rows(wc_raw[1], wc, *wc_cols[1])
-        load_rows(wc_raw[2], wc, *wc_cols[2])
-        load_scales(nc.sync, wa_s, wa_scales, 0)
-        nc.sync.dma_start(out=wa_w[:].bitcast(I32), in_=wa_words.rearrange("z p n t -> p z (n t)").bitcast(I32))
-        [load_scales(nc.sync, wa_s, wa_scales, r) for r in range(1, 4)]
-        load_xq(0, 0)
-        load_xq(0, 1)
-        load_fp4(wq_w, wq_words)
-        [load_xq(c, z) for c in range(1, CHUNKS) for z in range(PASSES)]
+        def round_to_bf16(on_vector, dst, src, lo, hi):
+            dst_view = dst[:, lo:hi, :].rearrange("i (v u) j -> i v j u", u=LINE)
+            src_view = src[:, :, lo:hi].rearrange("i j (v u) -> i v j u", u=LINE)
+            if on_vector:
+                nc.vector.tensor_copy(out=dst_view, in_=src_view)
+            else:
+                nc.scalar.activation(out=dst_view, in_=src_view, func=COPY)
 
-        def round_on_vector(grouped, raw, lo, hi):
-            dst, src = interleave_views(grouped, raw, lo, hi)
-            nc.vector.tensor_copy(out=dst, in_=src)
+        def quantise(words, scales, values):
+            nc.vector.quantize_mx(out=words.bitcast(FP8X4), scales=scales, in_=values.rearrange("i w j -> i (w j)"))
 
-        def round_on_scalar(grouped, raw, lo, hi):
-            dst, src = interleave_views(grouped, raw, lo, hi)
-            nc.scalar.activation(out=dst, in_=src, func=COPY)
+        def prepare_wc(i):
+            z, lo, hi = WC_PIECES[i]
+            split = int((hi - lo) * VECTOR_SHARE)
+            round_to_bf16(False, wc_bf[i], wc_raw[i], split, hi - lo)
+            round_to_bf16(True, wc_bf[i], wc_raw[i], 0, split)
+            quantise(wc_w[z][:, lo:hi], wc_s[z][:, lo:hi], wc_bf[i][:])
 
-        def quantise(words, scales, grouped):
-            nc.vector.quantize_mx(
-                out=words.bitcast(FP8X4), scales=scales, in_=grouped[:].rearrange("p w j -> p (w j)")
-            )
+        def round_xq(on_vector, c, z):
+            round_to_bf16(on_vector, xq_bf[c, z], xq_raw[c, z], 0, CHUNK)
 
-        def round_wc(i):
-            z, lo, hi = wc_cols[i]
-            width = hi - lo
-            split = width * 11 // 16
-            round_on_scalar(wc_bf[i], wc_raw[i], split, width)
-            round_on_vector(wc_bf[i], wc_raw[i], 0, split)
-
-        def quantise_wc(i):
-            z, lo, hi = wc_cols[i]
-            quantise(wc_w[z][:, lo:hi], wc_s[z][:, lo:hi], wc_bf[i])
-
-        def quantise_xq(c, z):
-            quantise(xq_w[c, z][:], xq_s[c, z][:], xq_bf[c, z])
-
-        def xa_pass(acc, c, z, words, scales, start, stop):
+        def xa_pass(acc, c, z, words, scales, stop):
             nc.tensor.matmul_mx(
                 out=acc[:],
                 lhsT=xa_w[:, z, 2 * c * CHUNK : 2 * (c + 1) * CHUNK].bitcast(FP4X4),
                 lhsT_scale=xa_s[:, z, c * CHUNK : (c + 1) * CHUNK],
                 rhs=words.bitcast(FP8X4),
                 rhs_scale=scales,
-                start=start,
+                start=(z == 0),
                 stop=stop,
             )
 
+        def wa_passes(c):
+            for z in range(PASSES):
+                xa_pass(p_acc[c], c, z, wa_w[:, z, :], wa_s[:, z, :], False)
+
+        def wc_passes(z):
+            for c in range(CHUNKS):
+                xa_pass(r_acc[c], c, z, wc_w[z][:], wc_s[z][:], z == PASSES - 1)
+
         def xq_pass(c, z):
+            quantise(xq_w[c, z][:], xq_s[c, z][:], xq_bf[c, z][:])
             nc.tensor.matmul_mx(
                 out=p_acc[c][:],
                 lhsT=xq_w[c, z][:].bitcast(FP8X4),
@@ -157,145 +142,125 @@ def tile_mix_larger_of_two_sums_pl_kernel(
             )
 
         def dealt(acc):
-            return acc[:].rearrange("t (m r) -> t r m", r=PACK)
-
-        def copy_r(c):
-            nc.scalar.activation(out=rn[c][:], in_=dealt(r_acc[c]), func=COPY, scale=-0.25)
+            return acc[:].rearrange("t (m j) -> t j m", j=PACK)
 
         def take_larger(c):
             nc.vector.scalar_tensor_tensor(
-                out=larger[c][:], in0=rn[c][:], scalar=-5.6, in1=dealt(p_acc[c]), op0=ALU.mult, op1=ALU.max
+                out=larger[c][:], in0=r_quarter[c][:], scalar=-5.6, in1=dealt(p_acc[c]), op0=ALU.mult, op1=ALU.max
             )
 
         def take_both(c):
             nc.vector.scalar_tensor_tensor(
-                out=both[c][:], in0=dealt(p_acc[c]), scalar=-0.25, in1=rn[c][:], op0=ALU.mult, op1=ALU.add
+                out=both[c][:], in0=dealt(p_acc[c]), scalar=-0.25, in1=r_quarter[c][:], op0=ALU.mult, op1=ALU.add
             )
 
-        def turn(c, i):
-            if i == 0:
-                y_acc[c] = ps.tile([P, PACK, CHUNK], F32, name="y_acc%d" % c, tag="r%d" % c)
-            term = (larger, both)[i][c]
-            for r in range(PACK):
-                nc.tensor.matmul(
-                    out=y_acc[c][:, r, :],
-                    lhsT=term[:, r, :],
-                    rhs=ident[:],
-                    is_transpose=True,
-                    start=(i == 0 and r == 0),
-                    stop=(i == 1 and r == PACK - 1),
-                )
+        def transpose_and_add(c):
+            y_acc[c] = psum.tile([P, PACK, CHUNK], F32, name="y_acc%d" % c, tag="r%d" % c)
+            for term in (larger, both):
+                for j in range(PACK):
+                    nc.tensor.matmul(
+                        out=y_acc[c][:, j, :],
+                        lhsT=term[c][:, j, :],
+                        rhs=identity[:],
+                        is_transpose=True,
+                        start=(term is larger and j == 0),
+                        stop=(term is both and j == PACK - 1),
+                    )
 
-        out_rows = out_0.rearrange("(p r) t -> p r t", r=PACK)
-        out_words = out_1[0].rearrange("p c r -> p (c r)").bitcast(I32)
+        out_rows = out_0.rearrange("(i j) t -> i j t", j=PACK)
+        out_words = out_1[0].rearrange("i t j -> i (t j)").bitcast(I32)
 
-        def copy_y(c):
-            nc.scalar.copy(out=y[c][:], in_=y_acc[c][:])
+        def copy_y(c, lo, hi):
+            nc.scalar.copy(out=y[c][:, :, lo:hi], in_=y_acc[c][:, :, lo:hi])
+
+        def store_y(c):
             nc.sync.dma_start(out=out_rows[:, :, c * CHUNK : (c + 1) * CHUNK], in_=y[c][:])
 
-        def round_y(c, lo=0, hi=CHUNK):
-            round_on_vector(y_bf[c], y[c], lo, hi)
+        def round_y(on_vector, c, lo, hi):
+            round_to_bf16(on_vector, y_bf[c], y[c], lo, hi)
 
-        def quantise_y(c, lo=0, hi=CHUNK):
+        def quantise_y(c, lo, hi):
             cols = slice(c * CHUNK + lo, c * CHUNK + hi)
             quantise(y_w[:, cols], y_s[:, cols], y_bf[c][:, lo:hi, :])
 
-        def copy_y_halves(c):
-            for lo in (0, CHUNK // 2):
-                cols = slice(lo, lo + CHUNK // 2)
-                nc.scalar.copy(out=y[c][:, :, cols], in_=y_acc[c][:, :, cols])
+        def store_words(lo, hi):
+            nc.sync.dma_start(out=out_words[:, lo:hi], in_=y_w[:, lo:hi].bitcast(I32))
 
-        def round_xq(c, z):
-            round_on_scalar(xq_bf[c, z], xq_raw[c, z], 0, CHUNK)
+        for scales_tile in (wq_s, xa_s, wa_s):
+            nc.vector.memset(scales_tile[:].bitcast(I32), 0)
 
-        def a_pass(c, z):
-            xa_pass(p_acc[c], c, z, wa_w[:, z, :], wa_s[:, z, :], z == 0, False)
+        for s in range(SCALE_ROWS):
+            load_scales(nc.gpsimd, wq_s, wq_scales, s)
+        make_identity(nc, identity[:])
+        load_rows(wc_raw[0], wc, *WC_PIECES[0])
+        load_words(xa_w, xa_words.rearrange("z i b -> i z b"))
+        for s in range(SCALE_ROWS):
+            load_scales(nc.sync, xa_s, xa_scales, s)
+        load_rows(wc_raw[1], wc, *WC_PIECES[1])
+        load_rows(wc_raw[2], wc, *WC_PIECES[2])
+        load_scales(nc.sync, wa_s, wa_scales, 0)
+        load_words(wa_w, wa_words.rearrange("z i n j -> i z (n j)"))
+        for s in range(1, SCALE_ROWS):
+            load_scales(nc.sync, wa_s, wa_scales, s)
+        for z in range(PASSES):
+            load_xq(0, z)
+        load_words(wq_w, wq_words.rearrange("z i b -> i z b"))
+        for c, z in xq_pieces[PASSES:]:
+            load_xq(c, z)
 
-        def r_pass(c, z):
-            xa_pass(r_acc[c], c, z, wc_w[z][:], wc_s[z][:], z == 0, z == 1)
+        prepare_wc(0)
+        wc_passes(0)
+        prepare_wc(1)
+        prepare_wc(2)
+        wc_passes(1)
+        for c in range(CHUNKS):
+            nc.scalar.activation(out=r_quarter[c][:], in_=dealt(r_acc[c]), func=COPY, scale=-0.25)
 
-        def round_y_s(c):
-            round_on_scalar(y_bf[c], y[c], 0, CHUNK)
+        wa_passes(0)
+        wa_passes(1)
+        for z in range(PASSES):
+            round_xq(True, 0, z)
+        for z in range(PASSES):
+            xq_pass(0, z)
+        wa_passes(2)
+        wa_passes(3)
 
-        def round_xq_v(c, z):
-            round_on_vector(xq_bf[c, z], xq_raw[c, z], 0, CHUNK)
+        for c in range(CHUNKS):
+            if c < LAST:
+                round_xq(c == 0, c + 1, 0)
+                round_xq(False, c + 1, 1)
+            if c >= 2:
+                copy_y(c - 2, 0, CHUNK)
+                store_y(c - 2)
+            if c < LAST:
+                xq_pass(c + 1, 0)
+            else:
+                round_y(False, 0, 0, CHUNK)
+            take_larger(c)
+            if c < LAST:
+                xq_pass(c + 1, 1)
+            take_both(c)
+            transpose_and_add(c)
 
-        round_wc(0)
-        quantise_wc(0)
-        [r_pass(c, 0) for c in range(CHUNKS)]
-        round_wc(1)
-        quantise_wc(1)
-        round_wc(2)
-        quantise_wc(2)
-        [r_pass(c, 1) for c in range(CHUNKS)]
-        [copy_r(c) for c in range(CHUNKS)]
-        a_pass(0, 0)
-        a_pass(0, 1)
-        a_pass(1, 0)
-        a_pass(1, 1)
-        round_xq_v(0, 0)
-        round_xq_v(0, 1)
-        quantise_xq(0, 0)
-        quantise_xq(0, 1)
-        xq_pass(0, 0)
-        xq_pass(0, 1)
-        a_pass(2, 0)
-        a_pass(2, 1)
-        a_pass(3, 0)
-        round_xq(1, 0)
-        round_xq(1, 1)
-        take_larger(0)
-        quantise_xq(1, 0)
-        xq_pass(1, 0)
-        take_both(0)
-        quantise_xq(1, 1)
-        xq_pass(1, 1)
-        turn(0, 0)
-        turn(0, 1)
-        round_xq(2, 0)
-        round_xq(2, 1)
-        quantise_xq(2, 0)
-        xq_pass(2, 0)
-        take_larger(1)
-        quantise_xq(2, 1)
-        xq_pass(2, 1)
-        take_both(1)
-        a_pass(3, 1)
-        turn(1, 0)
-        turn(1, 1)
-        round_xq(3, 0)
-        round_xq(3, 1)
-        copy_y(0)
-        quantise_xq(3, 0)
-        xq_pass(3, 0)
-        take_larger(2)
-        quantise_xq(3, 1)
-        xq_pass(3, 1)
-        take_both(2)
-        turn(2, 0)
-        turn(2, 1)
-        copy_y(1)
-        round_y_s(0)
-        take_larger(3)
-        turn(3, 0)
-        take_both(3)
-        turn(3, 1)
-        copy_y(2)
-        round_y(1)
-        quantise_y(0)
-        copy_y_halves(3)
-        round_y(2)
-        quantise_y(1)
-        nc.sync.dma_start(out=out_words[:, : 2 * CHUNK], in_=y_w[:, : 2 * CHUNK].bitcast(I32))
-        nc.sync.dma_start(out=out_rows[:, :, 3 * CHUNK :], in_=y[3][:])
-        quantise_y(2)
-        round_y(3, 0, 64)
-        round_y(3, 64, 128)
-        quantise_y(3, 0, 64)
-        quantise_y(3, 64, 128)
-        nc.sync.dma_start(out=out_words[:, 2 * CHUNK :], in_=y_w[:, 2 * CHUNK :].bitcast(I32))
-        for q in range(4):
-            queue = nc.scalar if q % 2 == 0 else nc.sync
-            queue.dma_start(
-                out=out_2[0, 4 * q : 4 * q + 4, :].bitcast(I32), in_=y_s[32 * q : 32 * q + 4, :].bitcast(I32)
-            )
+        halves = ((0, CHUNK // 2), (CHUNK // 2, CHUNK))
+        copy_y(LAST - 1, 0, CHUNK)
+        store_y(LAST - 1)
+        round_y(True, 1, 0, CHUNK)
+        quantise_y(0, 0, CHUNK)
+        for lo, hi in halves:
+            copy_y(LAST, lo, hi)
+        round_y(True, 2, 0, CHUNK)
+        quantise_y(1, 0, CHUNK)
+        store_words(0, T // 2)
+        store_y(LAST)
+        quantise_y(2, 0, CHUNK)
+        for lo, hi in halves:
+            round_y(True, LAST, lo, hi)
+        for lo, hi in halves:
+            quantise_y(LAST, lo, hi)
+        store_words(T // 2, T)
+        for quadrant in range(P // QUADRANT):
+            queue = nc.scalar if quadrant % 2 == 0 else nc.sync
+            rows = slice(SCALE_ROWS * quadrant, SCALE_ROWS * (quadrant + 1))
+            partitions = slice(QUADRANT * quadrant, QUADRANT * quadrant + SCALE_ROWS)
+            queue.dma_start(out=out_2[0, rows, :].bitcast(I32), in_=y_s[partitions, :].bitcast(I32))

from contextlib import ExitStack

import concourse.mybir as mybir
from concourse.masks import make_identity

K, L, T, N = 1024, 1024, 512, 512
FLOPS = 2 * N * T * (2 * K + L)

F32 = mybir.dt.float32
BF16 = mybir.dt.bfloat16
I32 = mybir.dt.int32
U32 = mybir.dt.uint32
U8 = mybir.dt.uint8
FP8X4 = mybir.dt.float8_e4m3fn_x4
FP4X4 = mybir.dt.float4_e2m1fn_x4
ALU = mybir.AluOpType
COPY = mybir.ActivationFunctionType.Copy

P = 128
PACK = 4
K_PASS = P * PACK
PASSES = K // K_PASS
QUADRANT = 32
SCALE_ROWS = 4
CHUNK = 128
CHUNKS = T // CHUNK
LAST = CHUNKS - 1
LINE = 4

WC_PIECES = ((0, 0, N), (1, 0, N // 2), (1, N // 2, N))
VECTOR_SHARE = 11 / 16


def tile_mix_larger_of_two_sums_pl_kernel(
    tc, xa_words, xa_scales, wa_words, wa_scales, xq, wq_words, wq_scales, wc, out_0, out_1, out_2
):
    nc = tc.nc
    with ExitStack() as ctx:
        sbuf = ctx.enter_context(tc.tile_pool(name="sbuf", bufs=1))
        psum = ctx.enter_context(tc.psum_pool(name="psum", bufs=1))
        ctx.enter_context(tc.manual_schedule())

        def tile(name, shape, dtype):
            return sbuf.tile(shape, dtype, name=name, align_bytes=64)

        xa_w = tile("xa_w", [P, PASSES, 2 * T], U8)
        wq_w = tile("wq_w", [P, PASSES, 2 * N], U8)
        wa_w = tile("wa_w", [P, PASSES, N], U32)
        xa_s = tile("xa_s", [P, PASSES, T], U8)
        wa_s = tile("wa_s", [P, PASSES, N], U8)
        wq_s = tile("wq_s", [P, PASSES, N], U8)
        identity = tile("identity", [P, P], F32)

        wc_raw = [tile("wc_raw%d" % i, [P, PACK, hi - lo], F32) for i, (z, lo, hi) in enumerate(WC_PIECES)]
        wc_bf = [tile("wc_bf%d" % i, [P, hi - lo, PACK], BF16) for i, (z, lo, hi) in enumerate(WC_PIECES)]
        wc_w = [tile("wc_w%d" % z, [P, N], U32) for z in range(PASSES)]
        wc_s = [tile("wc_s%d" % z, [P, N], U8) for z in range(PASSES)]
        xq_pieces = [(c, z) for c in range(CHUNKS) for z in range(PASSES)]
        xq_raw = {cz: tile("xq_raw%d%d" % cz, [P, PACK, CHUNK], F32) for cz in xq_pieces}
        xq_bf = {cz: tile("xq_bf%d%d" % cz, [P, CHUNK, PACK], BF16) for cz in xq_pieces}
        xq_w = {cz: tile("xq_w%d%d" % cz, [P, CHUNK], U32) for cz in xq_pieces}
        xq_s = {cz: tile("xq_s%d%d" % cz, [P, CHUNK], U8) for cz in xq_pieces}

        r_quarter = [tile("r_quarter%d" % c, [P, PACK, P], F32) for c in range(CHUNKS)]
        larger = [tile("larger%d" % c, [P, PACK, P], F32) for c in range(CHUNKS)]
        both = [tile("both%d" % c, [P, PACK, P], F32) for c in range(CHUNKS)]
        y = [tile("y%d" % c, [P, PACK, CHUNK], F32) for c in range(CHUNKS)]
        y_bf = [tile("y_bf%d" % c, [P, CHUNK, PACK], BF16) for c in range(CHUNKS)]
        y_w = tile("y_w", [P, T], U32)
        y_s = tile("y_s", [P, T], U8)

        p_acc = [psum.tile([P, N], F32, name="p_acc%d" % c, tag="p%d" % c) for c in range(CHUNKS)]
        r_acc = [psum.tile([P, N], F32, name="r_acc%d" % c, tag="r%d" % c) for c in range(CHUNKS)]
        y_acc = {}

        def load_scales(queue, dst, scales, s):
            queue.dma_start(
                out=dst[s:P:QUADRANT, :, :].bitcast(I32),
                in_=scales[:, s::SCALE_ROWS, :].rearrange("z q n -> q z n").bitcast(I32),
            )

        def load_words(dst, words):
            nc.sync.dma_start(out=dst[:].bitcast(I32), in_=words.bitcast(I32))

        def load_rows(dst, src, z, lo, hi):
            rows = src[z * K_PASS : (z + 1) * K_PASS, lo:hi]
            nc.sync.dma_start(out=dst[:], in_=rows.rearrange("(i j) w -> i j w", j=PACK))

        def load_xq(c, z):
            load_rows(xq_raw[c, z], xq, z, c * CHUNK, (c + 1) * CHUNK)

        def round_to_bf16(on_vector, dst, src, lo, hi):
            dst_view = dst[:, lo:hi, :].rearrange("i (v u) j -> i v j u", u=LINE)
            src_view = src[:, :, lo:hi].rearrange("i j (v u) -> i v j u", u=LINE)
            if on_vector:
                nc.vector.tensor_copy(out=dst_view, in_=src_view)
            else:
                nc.scalar.activation(out=dst_view, in_=src_view, func=COPY)

        def quantise(words, scales, values):
            nc.vector.quantize_mx(out=words.bitcast(FP8X4), scales=scales, in_=values.rearrange("i w j -> i (w j)"))

        def prepare_wc(i):
            z, lo, hi = WC_PIECES[i]
            split = int((hi - lo) * VECTOR_SHARE)
            round_to_bf16(False, wc_bf[i], wc_raw[i], split, hi - lo)
            round_to_bf16(True, wc_bf[i], wc_raw[i], 0, split)
            quantise(wc_w[z][:, lo:hi], wc_s[z][:, lo:hi], wc_bf[i][:])

        def round_xq(on_vector, c, z):
            round_to_bf16(on_vector, xq_bf[c, z], xq_raw[c, z], 0, CHUNK)

        def xa_pass(acc, c, z, words, scales, stop):
            nc.tensor.matmul_mx(
                out=acc[:],
                lhsT=xa_w[:, z, 2 * c * CHUNK : 2 * (c + 1) * CHUNK].bitcast(FP4X4),
                lhsT_scale=xa_s[:, z, c * CHUNK : (c + 1) * CHUNK],
                rhs=words.bitcast(FP8X4),
                rhs_scale=scales,
                start=(z == 0),
                stop=stop,
            )

        def wa_passes(c):
            for z in range(PASSES):
                xa_pass(p_acc[c], c, z, wa_w[:, z, :], wa_s[:, z, :], False)

        def wc_passes(z):
            for c in range(CHUNKS):
                xa_pass(r_acc[c], c, z, wc_w[z][:], wc_s[z][:], z == PASSES - 1)

        def xq_pass(c, z):
            quantise(xq_w[c, z][:], xq_s[c, z][:], xq_bf[c, z][:])
            nc.tensor.matmul_mx(
                out=p_acc[c][:],
                lhsT=xq_w[c, z][:].bitcast(FP8X4),
                lhsT_scale=xq_s[c, z][:],
                rhs=wq_w[:, z, :].bitcast(FP4X4),
                rhs_scale=wq_s[:, z, :],
                start=False,
                stop=(z == PASSES - 1),
            )

        def dealt(acc):
            return acc[:].rearrange("t (m j) -> t j m", j=PACK)

        def take_larger(c):
            nc.vector.scalar_tensor_tensor(
                out=larger[c][:], in0=r_quarter[c][:], scalar=-5.6, in1=dealt(p_acc[c]), op0=ALU.mult, op1=ALU.max
            )

        def take_both(c):
            nc.vector.scalar_tensor_tensor(
                out=both[c][:], in0=dealt(p_acc[c]), scalar=-0.25, in1=r_quarter[c][:], op0=ALU.mult, op1=ALU.add
            )

        def transpose_and_add(c):
            y_acc[c] = psum.tile([P, PACK, CHUNK], F32, name="y_acc%d" % c, tag="r%d" % c)
            for term in (larger, both):
                for j in range(PACK):
                    nc.tensor.matmul(
                        out=y_acc[c][:, j, :],
                        lhsT=term[c][:, j, :],
                        rhs=identity[:],
                        is_transpose=True,
                        start=(term is larger and j == 0),
                        stop=(term is both and j == PACK - 1),
                    )

        out_rows = out_0.rearrange("(i j) t -> i j t", j=PACK)
        out_words = out_1[0].rearrange("i t j -> i (t j)").bitcast(I32)

        def copy_y(c, lo, hi):
            nc.scalar.copy(out=y[c][:, :, lo:hi], in_=y_acc[c][:, :, lo:hi])

        def store_y(c):
            nc.sync.dma_start(out=out_rows[:, :, c * CHUNK : (c + 1) * CHUNK], in_=y[c][:])

        def round_y(on_vector, c, lo, hi):
            round_to_bf16(on_vector, y_bf[c], y[c], lo, hi)

        def quantise_y(c, lo, hi):
            cols = slice(c * CHUNK + lo, c * CHUNK + hi)
            quantise(y_w[:, cols], y_s[:, cols], y_bf[c][:, lo:hi, :])

        def store_words(lo, hi):
            nc.sync.dma_start(out=out_words[:, lo:hi], in_=y_w[:, lo:hi].bitcast(I32))

        for scales_tile in (wq_s, xa_s, wa_s):
            nc.vector.memset(scales_tile[:].bitcast(I32), 0)

        for s in range(SCALE_ROWS):
            load_scales(nc.gpsimd, wq_s, wq_scales, s)
        make_identity(nc, identity[:])
        load_rows(wc_raw[0], wc, *WC_PIECES[0])
        load_words(xa_w, xa_words.rearrange("z i b -> i z b"))
        for s in range(SCALE_ROWS):
            load_scales(nc.sync, xa_s, xa_scales, s)
        load_rows(wc_raw[1], wc, *WC_PIECES[1])
        load_rows(wc_raw[2], wc, *WC_PIECES[2])
        load_scales(nc.sync, wa_s, wa_scales, 0)
        load_words(wa_w, wa_words.rearrange("z i n j -> i z (n j)"))
        for s in range(1, SCALE_ROWS):
            load_scales(nc.sync, wa_s, wa_scales, s)
        for z in range(PASSES):
            load_xq(0, z)
        load_words(wq_w, wq_words.rearrange("z i b -> i z b"))
        for c, z in xq_pieces[PASSES:]:
            load_xq(c, z)

        prepare_wc(0)
        wc_passes(0)
        prepare_wc(1)
        prepare_wc(2)
        wc_passes(1)
        for c in range(CHUNKS):
            nc.scalar.activation(out=r_quarter[c][:], in_=dealt(r_acc[c]), func=COPY, scale=-0.25)

        wa_passes(0)
        wa_passes(1)
        for z in range(PASSES):
            round_xq(True, 0, z)
        for z in range(PASSES):
            xq_pass(0, z)
        wa_passes(2)
        wa_passes(3)

        for c in range(CHUNKS):
            if c < LAST:
                round_xq(c == 0, c + 1, 0)
                round_xq(False, c + 1, 1)
            if c >= 2:
                copy_y(c - 2, 0, CHUNK)
                store_y(c - 2)
            if c < LAST:
                xq_pass(c + 1, 0)
            else:
                round_y(False, 0, 0, CHUNK)
            take_larger(c)
            if c < LAST:
                xq_pass(c + 1, 1)
            take_both(c)
            transpose_and_add(c)

        halves = ((0, CHUNK // 2), (CHUNK // 2, CHUNK))
        copy_y(LAST - 1, 0, CHUNK)
        store_y(LAST - 1)
        round_y(True, 1, 0, CHUNK)
        quantise_y(0, 0, CHUNK)
        for lo, hi in halves:
            copy_y(LAST, lo, hi)
        round_y(True, 2, 0, CHUNK)
        quantise_y(1, 0, CHUNK)
        store_words(0, T // 2)
        store_y(LAST)
        quantise_y(2, 0, CHUNK)
        for lo, hi in halves:
            round_y(True, LAST, lo, hi)
        for lo, hi in halves:
            quantise_y(LAST, lo, hi)
        store_words(T // 2, T)
        for quadrant in range(P // QUADRANT):
            queue = nc.scalar if quadrant % 2 == 0 else nc.sync
            rows = slice(SCALE_ROWS * quadrant, SCALE_ROWS * (quadrant + 1))
            partitions = slice(QUADRANT * quadrant, QUADRANT * quadrant + SCALE_ROWS)
            queue.dma_start(out=out_2[0, rows, :].bitcast(I32), in_=y_s[partitions, :].bitcast(I32))
